import numpy as np
import ml_dtypes


def mxq(x, axis, fmt="e4m3"):
    dtype, down = {"e4m3": (ml_dtypes.float8_e4m3fn, 7), "e5m2": (ml_dtypes.float8_e5m2, 14)}[fmt]
    v = np.moveaxis(np.asarray(x, np.float32).astype(ml_dtypes.bfloat16).astype(np.float64), axis, -1)
    blocks = v.reshape(v.shape[:-1] + (-1, 32))
    amax = np.abs(blocks).max(-1, keepdims=True)
    byte = np.maximum(np.where(amax > 0, np.frexp(amax)[1] - 1 + 127, 0) - down, 1)
    scale = np.exp2(byte - 127.0)
    codes = (blocks / scale).astype(np.float32).astype(dtype).astype(np.float64)
    return np.moveaxis((codes * scale).reshape(v.shape), -1, axis)


WIDE = False


def mx_kscale(k):
    if not WIDE:
        return np.ones(k)
    levels = np.array([30, -30])
    if k % 512:
        return np.exp2(np.random.permutation(np.resize(levels, k // 32))).repeat(32)
    a = np.empty((k // 512, 16))
    for p in range(k // 512):
        a[p, :8] = np.random.permutation(np.resize(levels, 8))
        for g in range(8):
            far = levels[np.abs(levels - a[p, g]) >= 10]
            a[p, g + 8] = far[np.random.randint(len(far))]
    return np.exp2(a.ravel()).repeat(32)


BF16 = ml_dtypes.bfloat16


def bf(x):
    return np.asarray(x, np.float32).astype(BF16)


def f64(x):
    return np.asarray(x).astype(np.float64)


E2M1 = np.array([0.0, 0.5, 1.0, 1.5, 2.0, 3.0, 4.0, 6.0, -0.0, -0.5, -1.0, -1.5, -2.0, -3.0, -4.0, -6.0])


def pack_weight(w, fmt):
    k, n = w.shape
    w = f64(bf(w)).reshape(k // 32, 32, n)
    amax = np.abs(w).max(1)
    if fmt in ("e4m3", "e5m2"):
        byte = np.frexp(amax)[1] - 1 + 127 - (7 if fmt == "e4m3" else 14)
    else:
        mant, ex = np.frexp(amax / 6.0)
        byte = np.where(mant > 0.5, ex, ex - 1) + 127
    byte = np.clip(np.where(amax > 0, byte, 1), 1, 254)
    scaled = (w * np.exp2(127.0 - byte)[:, None, :]).reshape(k, n).astype(np.float32)
    by_word = np.ascontiguousarray(scaled.reshape(k // 512, 128, 4, n).transpose(0, 1, 3, 2))
    if fmt in ("e4m3", "e5m2"):
        words = by_word.astype(ml_dtypes.float8_e4m3fn if fmt == "e4m3" else ml_dtypes.float8_e5m2).view(np.uint8)
    else:
        c = by_word.astype(ml_dtypes.float4_e2m1fn).view(np.uint8) & 0xF
        words = c[..., 0::2] | (c[..., 1::2] << 4)
    return np.ascontiguousarray(words), np.ascontiguousarray(byte.astype(np.uint8).reshape(k // 512, 16, n))


def unpack_weight(words, scales, fmt):
    g, p, n, _ = words.shape
    if fmt in ("e4m3", "e5m2"):
        vals = np.ascontiguousarray(words).view(ml_dtypes.float8_e4m3fn if fmt == "e4m3" else ml_dtypes.float8_e5m2).astype(np.float64)
    else:
        nib = np.empty((g, p, n, 4), np.uint8)
        nib[..., 0::2] = words & 0xF
        nib[..., 1::2] = words >> 4
        vals = E2M1[nib]
    vals = vals * np.repeat(np.exp2(scales.astype(np.float64) - 127.0), 8, axis=1)[..., None]
    return vals.transpose(0, 1, 3, 2).reshape(g * 512, n)

def planes(Y):
    n, m = Y.shape
    b = f64(bf(Y)).reshape(n // 32, 32, m)
    amax = np.abs(b).max(1)
    byte = np.clip(np.where(amax > 0, np.frexp(amax)[1] - 1 + 127 - 7, 1), 1, 254)
    codes = (b * np.exp2(127.0 - byte)[:, None, :]).reshape(n, m).astype(np.float32).astype(ml_dtypes.float8_e4m3fn).view(np.uint8)
    words = codes.reshape(n // 512, 128, 4, m).transpose(0, 1, 3, 2)
    return np.ascontiguousarray(words), np.ascontiguousarray(byte.astype(np.uint8).reshape(n // 512, 16, m))


I, J, C, D = 1536, 2048, 1024, 16

def setup_inputs():
    unit = 0.25 * np.exp(0.8 * np.random.randn(C))
    X = np.random.randn(J, C) * unit
    beta = 2.0 * np.random.randn(C) / (np.sqrt(C) * unit)
    eta = (X * beta).sum(axis=1)
    h = np.exp(eta - eta.max())
    h = h * (3.0 * D / h.sum())
    A = np.random.rand(I, J) ** 2
    d = np.random.randint(D // 2, D + D // 2 + 1, I)
    events = np.stack([X[np.random.permutation(J)[:n]].sum(axis=0) for n in d])
    jump = d / (A * h).sum(axis=1)
    s = mx_kscale(J)
    g_words, g_scales = pack_weight(h[:, None] * X / s[:, None], "e5m2")
    return {"atrisk": bf(A * s), "g_words": g_words, "g_scales": g_scales,
            "events": bf(events), "jump": bf(jump)}

def reference(atrisk, g_words, g_scales, events, jump):
    A = mxq(f64(atrisk), 1, "e4m3")
    G = unpack_weight(g_words, g_scales, "e5m2")
    S1 = A @ G
    y = f64(events) - f64(jump)[:, None] * S1
    Y = y.T
    words, scales = planes(Y)
    return y, words, scales

from contextlib import ExitStack

import concourse.mybir as mybir
from concourse.masks import make_identity

I, J, C = 1536, 2048, 1024
FLOPS = 2 * I * J * C

F32 = mybir.dt.float32
BF16 = mybir.dt.bfloat16
I32 = mybir.dt.int32
U32 = mybir.dt.uint32
U8 = mybir.dt.uint8
E4M3X4 = mybir.dt.float8_e4m3fn_x4
E5M2X4 = mybir.dt.float8_e5m2_x4
MULT = mybir.AluOpType.mult
ADD = mybir.AluOpType.add

P = 128
TILES = I // P
PASSES = J // 512
HALVES = C // 512
ACC_BANKS = 4
TURN_BANKS = 4
LAG = 3
FIRST_SPLIT = 5
WORD_RUNS = {0: [(0, 4), (4, 8), (8, 12)], 1: [(0, 4), (4, 8), (8, 10), (10, 12)]}
SCALE_RUNS = [(0, 7), (7, 12)]


def pinned_order(do):
    last = TILES - 1
    do("load_jump")
    do("load_a", 0, 0, 2)
    do("load_g_scales", 0)
    do("load_a", 0, 2, 4)
    do("load_g_words", 0, 0)
    do("load_a", 1, 0, 4)
    for g in range(1, PASSES):
        do("load_g_words", g, 0)
    do("load_a", 2, 0, 4)
    do("load_a", 3, 0, 4)
    do("load_events", 0, 0, 1)
    do("load_events", 1, 0, 1)
    do("load_g_scales", 1)
    do("load_a", 4, 0, 4)
    do("load_events", 2, 0, 1)
    for g in range(PASSES):
        do("load_g_words", g, 1)
    for t in range(LAG, TILES + LAG):
        if t + 2 < TILES:
            do("load_a", t + 2, 0, 4)
        if t < TILES:
            do("load_events", t, 0, 1)
        do("load_events", t - LAG, 1, 2)

    def planes(units):
        for t, h in units:
            do("quant_y", t, h)
        for t, h in units:
            for t0, t1 in WORD_RUNS[h]:
                if t1 - 1 == t:
                    do("store_words", h, t0, t1)
            for t0, t1 in SCALE_RUNS:
                if t1 - 1 == t and h == 1:
                    do("store_scales", t0, t1)

    def finish(t, h):
        do("finish", t, h)
        do("store_y", t, h)

    for kh in range(2):
        do("turn_a", 0, kh)
        do("lay_a", 0, kh, "S")
        do("quant_a", 0, kh)
    for t in range(TILES):
        b = t - LAG
        ahead = t + 1 < TILES
        back = tuple((u, h) for u, h in ((t - 2, 0), (b - 2, 1)) if u >= 0)
        if t == 0:
            do("multiply", 0, 0, 0, 1)
        if ahead:
            do("turn_a", t + 1, 0)
            do("turn_a", t + 1, 1)
        if t == 1:
            do("spread_jump")
        if back:
            do("turn_y", back)
        if ahead:
            do("lay_a", t + 1, 0, "S")
        if b >= 1:
            finish(b - 1, 1)
        if ahead:
            do("quant_a", t + 1, 0)
            do("lay_a", t + 1, 1, "S")
        if t > LAG:
            do("round_y", t - 1, 0, "V")
        if ahead:
            do("quant_a", t + 1, 1)
        if 1 <= t <= LAG:
            finish(t - 1, 0)
        if b >= 1:
            do("round_y", b - 1, 1, "V")
        if back:
            do("lay_y", back, "S")
            planes(back)
        if 1 <= t <= LAG:
            do("round_y", t - 1, 0, "V")
        if FIRST_SPLIT <= t + 2 < TILES:
            do("split_a", t + 2, "S", 0, 3)
            do("split_a", t + 2, "V", 3, 4)
        do("multiply", t, 0, 1 if t == 0 else 0, 4)
        if b >= 0:
            do("multiply", b, 1, 0, 4)
        if t >= LAG:
            finish(t, 0)

    first = ((last - 1, 0), (last - 4, 1))
    second = ((last, 0), (last - 3, 1))
    third = ((last - 2, 1), (last - 1, 1))
    final = ((last, 1),)
    finish(last - 3, 1)
    do("round_y", last, 0, "V")
    do("multiply", last - 2, 1, 0, 4)
    do("multiply", last - 1, 1, 0, 4)
    do("round_y", last - 3, 1, "S")
    finish(last - 2, 1)
    do("round_y", last - 2, 1, "S")
    finish(last - 1, 1)
    do("turn_y", first)
    do("turn_y", second)
    do("round_y", last - 1, 1, "V")
    do("lay_y", first, "S")
    do("lay_y", second, "S")
    do("multiply", last, 1, 0, 4)
    planes(first)
    planes(second)
    do("turn_y", third)
    do("lay_y", third, "S")
    do("finish_bf16", last, 1)
    do("turn_y", final)
    finish(last, 1)
    do("lay_y", final, "S")
    planes(third)
    planes(final)


def tile_cox_interval_scores_k2_kernel(tc, atrisk, g_words, g_scales, events, jump, out_0, out_1, out_2):
    nc = tc.nc
    copy_on = {"S": nc.scalar.copy, "V": nc.vector.tensor_copy}

    with ExitStack() as ctx:
        keep = ctx.enter_context(tc.tile_pool(name="keep", bufs=1))
        ring = ctx.enter_context(tc.tile_pool(name="ring", bufs=4))
        acc_pool = ctx.enter_context(tc.psum_pool(name="acc", bufs=ACC_BANKS))
        turn_pool = ctx.enter_context(tc.psum_pool(name="turn", bufs=TURN_BANKS))
        ctx.enter_context(tc.manual_schedule())

        ident = keep.tile([P, P], F32, name="ident")
        jump_rows = keep.tile([P, P], BF16, name="jump_rows")
        jump_neg = keep.tile([P, P], F32, name="jump_neg")
        minus_jump = keep.tile([P, TILES], F32, name="minus_jump")
        a_raw = [keep.tile([P, J], BF16, name="a_raw%d" % t) for t in range(TILES)]
        ev = [[keep.tile([P, 512], BF16, name="ev%d_%d" % (t, h)) for h in range(HALVES)] for t in range(TILES)]
        y = [[keep.tile([P, 512], F32, name="y%d_%d" % (t, h)) for h in range(HALVES)] for t in range(TILES)]
        gw = [[keep.tile([P, 512], U32, name="gw%d_%d" % (g, h), align_bytes=64) for h in range(HALVES)] for g in range(PASSES)]
        gs = [keep.tile([P, PASSES, 512], U8, name="gs%d" % h, align_bytes=64) for h in range(HALVES)]
        y_codes = {}
        for h in range(HALVES):
            for t0, t1 in WORD_RUNS[h]:
                run = keep.tile([P, (t1 - t0) * P], U32, name="y_codes%d_%d" % (t0, h), align_bytes=64)
                for t in range(t0, t1):
                    y_codes[t, h] = (run, (t - t0) * P)
        y_scales = {}
        for t0, t1 in SCALE_RUNS:
            run = keep.tile([P, HALVES, (t1 - t0) * P], U8, name="y_scales%d" % t0, align_bytes=64)
            for t in range(t0, t1):
                y_scales[t] = (run, (t - t0) * P)
        live = {}

        def rows(t):
            return slice(t * P, (t + 1) * P)

        def load_jump():
            nc.scalar.dma_start(out=jump_rows[0:TILES, :], in_=jump.rearrange("(t p) -> t p", p=P))

        def load_a(t, g0, g1):
            nc.sync.dma_start(out=a_raw[t][:, 512 * g0 : 512 * g1], in_=atrisk[rows(t), 512 * g0 : 512 * g1])

        def load_g_scales(h):
            for q in range(4):
                src = g_scales[:, 4 * q : 4 * q + 4, 512 * h : 512 * (h + 1)].rearrange("g r n -> r g n")
                nc.sync.dma_start(out=gs[h][32 * q : 32 * q + 4, :, :].bitcast(I32), in_=src.bitcast(I32))

        def load_g_words(g, h):
            src = g_words[g].rearrange("p n t -> p (n t)")[:, 2048 * h : 2048 * (h + 1)]
            nc.sync.dma_start(out=gw[g][h][:].bitcast(I32), in_=src.bitcast(I32))

        def load_events(t, h0, h1):
            nc.sync.dma_start(out=ev[t][h0][:], in_=events[rows(t), 512 * h0 : 512 * h1])

        def spread_jump():
            nc.vector.tensor_scalar(jump_neg[:], jump_rows[:], -1.0, None, MULT)
            bank = turn_pool.tile([P, 4, P], F32, name="bank")
            nc.tensor.transpose(bank[:, 0, :], jump_neg[:], ident[:])
            nc.vector.tensor_copy(out=minus_jump[:], in_=bank[:, 0, 0:TILES])

        def split_a(t, engine, g0, g1):
            if ("split", t) not in live:
                live["split", t] = ring.tile([P, PASSES, 2, P], F32, name="a_split", bufs=2)
            words = a_raw[t][:].bitcast(F32)[:, 256 * g0 : 256 * g1]
            copy_on[engine](out=live["split", t][:, g0:g1, :, :], in_=words.rearrange("p (g q u) -> p g u q", q=P, u=2))

        def turn_a(t, kh):
            bank = turn_pool.tile([P, 4, P], F32, name="bank")
            live["a_bank", t, kh] = bank
            words = a_raw[t][:].bitcast(F32)
            for g in (2 * kh, 2 * kh + 1):
                for u in range(2):
                    if ("split", t) in live:
                        src = live["split", t][:, g, u, :]
                    else:
                        src = words[:, 256 * g + u : 256 * (g + 1) : 2]
                    nc.tensor.transpose(bank[:, 2 * (g % 2) + u, :], src, ident[:])

        def lay_a(t, kh, engine):
            laid = ring.tile([P, 1024], BF16, name="a_laid", align_bytes=64)
            live["a_laid", t, kh] = laid
            copy_on[engine](
                out=laid[:].bitcast(F32).rearrange("p (g r u) -> p g r u", g=2, u=2),
                in_=live["a_bank", t, kh][:].rearrange("p (g u) r -> p g r u", u=2),
            )

        def quant_a(t, kh):
            codes = ring.tile([P, 2 * P], U32, name="a_codes", align_bytes=64, bufs=2 * (LAG + 3))
            scales = ring.tile([P, 2 * P], U8, name="a_scales", align_bytes=64, bufs=2 * (LAG + 3))
            live["a_mx", t, kh] = (codes, scales)
            nc.vector.quantize_mx(out=codes[:].bitcast(E4M3X4), scales=scales[:], in_=live["a_laid", t, kh][:])

        def multiply(t, h, g0, g1):
            if g0 == 0:
                live["acc", t, h] = acc_pool.tile([P, 512], F32, name="acc")
            for g in range(g0, g1):
                codes, scales = live["a_mx", t, g // 2]
                cols = slice(P * (g % 2), P * (g % 2 + 1))
                nc.tensor.matmul_mx(
                    out=live["acc", t, h][:],
                    lhsT=codes[:, cols].bitcast(E4M3X4),
                    lhsT_scale=scales[:, cols],
                    rhs=gw[g][h][:].bitcast(E5M2X4),
                    rhs_scale=gs[h][:, g, :],
                    start=(g == 0),
                    stop=(g == PASSES - 1),
                )

        def score(t, h, out):
            nc.vector.scalar_tensor_tensor(out, live["acc", t, h][:], minus_jump[:, t : t + 1], ev[t][h][:], MULT, ADD)

        def finish(t, h):
            score(t, h, y[t][h][:])

        def finish_bf16(t, h):
            rounded = ring.tile([P, 512], BF16, name="y_rounded", bufs=6)
            live["y_plain", t, h] = rounded
            score(t, h, rounded[:])

        def round_y(t, h, engine):
            rounded = ring.tile([P, 512], BF16, name="y_rounded", bufs=6)
            live["y_split", t, h] = rounded
            copy_on[engine](
                out=rounded[:].rearrange("p (u q e) -> p u q e", u=2, e=2),
                in_=y[t][h][:].rearrange("p (q u e) -> p u q e", u=2, e=2),
            )

        def turn_y(units):
            bank = turn_pool.tile([P, 4, P], F32, name="bank")
            live["y_bank", units] = bank
            for n, (t, h) in enumerate(units):
                for u in range(2):
                    if ("y_split", t, h) in live:
                        src = live["y_split", t, h][:].bitcast(F32)[:, P * u : P * (u + 1)]
                    else:
                        src = live["y_plain", t, h][:].bitcast(F32)[:, u : 2 * P : 2]
                    nc.tensor.transpose(bank[:, 2 * n + u, :], src, ident[:])

        def lay_y(units, engine):
            laid = ring.tile([P, 1024], BF16, name="y_laid", align_bytes=64)
            count = len(units)
            for n, (t, h) in enumerate(units):
                live["y_laid", t, h] = laid[:, 512 * n : 512 * (n + 1)]
            copy_on[engine](
                out=laid[:, 0 : 512 * count].bitcast(F32).rearrange("p (n r u) -> p n r u", n=count, u=2),
                in_=live["y_bank", units][:, 0 : 2 * count, :].rearrange("p (n u) r -> p n r u", u=2),
            )

        def quant_y(t, h):
            codes, c0 = y_codes[t, h]
            scales, s0 = y_scales[t]
            nc.vector.quantize_mx(
                out=codes[:, c0 : c0 + P].bitcast(E4M3X4), scales=scales[:, h, s0 : s0 + P], in_=live["y_laid", t, h]
            )

        def store_y(t, h):
            nc.sync.dma_start(out=out_0[rows(t), 512 * h : 512 * (h + 1)], in_=y[t][h][:])

        def store_words(h, t0, t1):
            dst = out_1[h].rearrange("p m t -> p (m t)")[:, 4 * P * t0 : 4 * P * t1]
            nc.sync.dma_start(out=dst.bitcast(I32), in_=y_codes[t0, h][0][:].bitcast(I32))

        def store_scales(t0, t1):
            for q in range(4):
                dst = out_2[:, 4 * q : 4 * q + 4, P * t0 : P * t1].rearrange("g r m -> r g m")
                nc.sync.dma_start(out=dst.bitcast(I32), in_=y_scales[t0][0][32 * q : 32 * q + 4, :, :].bitcast(I32))

        steps = {
            "load_jump": load_jump, "load_a": load_a, "load_g_scales": load_g_scales, "load_g_words": load_g_words,
            "load_events": load_events, "spread_jump": spread_jump, "split_a": split_a, "turn_a": turn_a,
            "lay_a": lay_a, "quant_a": quant_a, "multiply": multiply, "finish": finish, "finish_bf16": finish_bf16,
            "round_y": round_y, "turn_y": turn_y, "lay_y": lay_y, "quant_y": quant_y, "store_y": store_y,
            "store_words": store_words, "store_scales": store_scales,
        }

        nc.vector.memset(gs[0][:].rearrange("p g n -> p (g n)").bitcast(I32), 0)
        nc.vector.memset(jump_rows[:], 0.0)
        nc.vector.memset(gs[1][:].rearrange("p g n -> p (g n)").bitcast(I32), 0)
        make_identity(nc, ident[:])
        pinned_order(lambda name, *args: steps[name](*args))
